import numpy as np, ml_dtypes
CORES = [88,96,104,112,120,216,224,232,240,248]
N = 10
KB, QP = 1, 256
MEM = [4,7,9]
def setup_inputs(rng):
    q = rng.standard_normal((N, 128, QP), dtype=np.float32) / 4; k = rng.standard_normal((N, 128, KB * 128), dtype=np.float32)
    a = 2 * np.pi * rng.random((N, QP)); s = 400 * rng.random((N, QP)) ** 1.5; q[:, 0, :] = s * np.cos(a); q[:, 1, :] = s * np.sin(a); q[:, 2, :] = 150 * rng.standard_normal((N, QP)); k[:, 2, :] = 1 + k[:, 2, :] / 50
    c = np.zeros(N); c[MEM] = rng.permutation(len(MEM))
    a = (2 * np.pi * rng.random() + np.pi / 2 * (c.reshape(N, 1, 1) + 0.5) / len(MEM) - 0.5 + (np.arange(KB).reshape(1, KB, 1) + rng.random((N, KB, 128))) / KB).reshape(N, KB * 128); k[:, 0, :] = np.cos(a); k[:, 1, :] = np.sin(a)
    return {"q": q.astype(ml_dtypes.bfloat16), "k": k.astype(ml_dtypes.bfloat16), "v": rng.standard_normal((N, 128, KB * 128), dtype=np.float32).astype(ml_dtypes.bfloat16)}
def setup_inputs_big(rng):
    d = setup_inputs(rng)
    for k in ("v",): d[k] = (d[k].astype(np.float32) * 1048576.0).astype(d[k].dtype)
    return d
def setup_inputs_small(rng):
    d = setup_inputs(rng)
    for k in ("v",): d[k] = (d[k].astype(np.float32) * (1 / 1048576.0)).astype(d[k].dtype)
    return d
def reference(q, k, v):
    Q, K, V = q.astype(np.float64), k.astype(np.float64), v.astype(np.float64)
    y = np.zeros((N, QP, 128))
    for r in range(N):
        js = list(MEM)
        S = np.concatenate([K[j].T @ Q[r] for j in js], axis=0)
        P = np.exp(S - S.max(axis=0)); P = P / P.sum(axis=0)
        y[r] = P.T @ np.concatenate([V[j][:, 128 * b:128 * b + 128] for j in js for b in range(KB)], axis=0)
    return {"y": y.astype(ml_dtypes.bfloat16)}

@@ -1,0 +1,235 @@
+from concourse.bass import DstId, RemoteDMATransfer
+from concourse.mybir import AluOpType, AxisListType, ActivationFunctionType
+
+NSIM = 256
+NENG = 16
+NE_SRC = 8
+NE_HLP = 8
+
+SCRATCH = {
+    "hkv": ("dram", [2, 128, 128], "bfloat16"),
+    "qsb": ("sbuf", [128, 256], "bfloat16"),
+    "kall": ("sbuf", [128, 384], "bfloat16"),
+    "vall": ("sbuf", [128, 384], "bfloat16"),
+    "idn": ("sbuf", [128, 128], "bfloat16"),
+    "pf": ("sbuf", [128, 256], "bfloat16"),
+    "p": ("sbuf", [128, 768], "bfloat16"),
+    "pts": ("sbuf", [128, 768], "bfloat16"),
+    "st": ("sbuf", [128, 64], "float32"),
+    "ysb": ("sbuf", [128, 256], "bfloat16"),
+    "sf0": ("psum", [128, 512], "float32"),
+    "sf1": ("psum", [128, 512], "float32"),
+    "s0": ("psum", [128, 512], "float32"),
+    "s1": ("psum", [128, 512], "float32"),
+    "pt0": ("psum", [128, 1024], "bfloat16"),
+    "pt1": ("psum", [128, 1024], "bfloat16"),
+    "o0": ("psum", [128, 512], "float32"),
+    "o1": ("psum", [128, 512], "float32"),
+}
+SEMAPHORES = (["sq", "sKL", "sVL", "loc", "sOne", "sI", "sL", "sR", "sD"]
+              + ["aK%d" % j for j in range(3)] + ["aV%d" % j for j in range(3)]
+              + [n + str(b) for n in ("sSF", "sS", "sMF", "sML", "sM", "sPF", "sW", "sP", "sPS", "sT", "sC", "sO", "sY")
+                 for b in range(2)])
+
+
+def _pick(mask, n):
+    m = 0
+    for i in [i for i in range(NENG) if (mask >> i) & 1][:n]:
+        m |= 1 << i
+    return m
+
+
+def _plan(T, topo):
+    cores = list(T.cores)
+    cnt = {}
+
+    def split(ds, own, other, n_own):
+        ds = sorted(ds, key=lambda d: cnt.get((d, own), 0) - cnt.get((d, other), 0))
+        a, b = ds[:n_own], ds[n_own:]
+        for d in a:
+            cnt[(d, own)] = cnt.get((d, own), 0) + 1
+        for d in b:
+            cnt[(d, other)] = cnt.get((d, other), 0) + 1
+        return a, b
+
+    plan = []
+    for j, r in enumerate(T.tables["MEM"]):
+        s = cores[r]
+        mates_on_chip = [c for c in range(NSIM) if c != s and topo.host(c) == topo.host(s)
+                         and topo.chip(c) == topo.chip(s) and T.rank_of(c) is None]
+        near = [d for d in cores if d != s and topo.may_write(s, d)]
+        far = [d for d in cores if d != s and not topo.may_write(s, d)]
+        own = topo.die(s)
+        other = [topo.die(c) for c in mates_on_chip if topo.die(c) != own][0]
+        port = [c for c in mates_on_chip if all(topo.may_write(c, d) for d in far)]
+        p_own = [c for c in port if topo.die(c) == own][0]
+        p_oth = [c for c in port if topo.die(c) == other][0]
+        x_oth = [c for c in mates_on_chip if topo.die(c) == other and c != p_oth and c not in port][0]
+        n_a, n_b = split(near, own, other, (len(near) + 1) // 2)
+        f_a, f_b = split(far, own, other, (len(far) + 1) // 2)
+        groups = [(s, n_a), (p_own, f_a), (p_oth, f_b), (x_oth, n_b)]
+        if j % 2:
+            groups = [(c, ds[::-1]) for c, ds in groups]
+        plan.append([(c, ds) for c, ds in groups if ds or c == s])
+    return plan
+
+
+def _send(g, T, topo, core, src, dests, dst_of, sem, ne):
+    m = (1 << NENG) - 1
+    ids, dsts = [], []
+    for d in dests:
+        m &= topo.mask(core, d)
+        rid, pid = topo.addr(d, core)
+        ids.append(DstId(rid=rid, pnc=pid))
+        dsts.append(dst_of)
+    g.remote_dma_fused([RemoteDMATransfer(dst_ids=ids, dma_engine_mask=_pick(m, ne), remote_sem=sem,
+                                          srcs=[src], dsts=dsts, alu_op=0)], local_sem=T.sem.loc)
+
+
+def rank_program(g, core, T, topo):
+    plan = _plan(T, topo)
+    S = T.sem
+    rank = T.rank_of(core)
+
+    if rank is None:
+        for j, groups in enumerate(plan):
+            for c, ds in groups[1:]:
+                if c != core:
+                    continue
+                g.wait_ge(S["aK%d" % j], NE_SRC)
+                _send(g, T, topo, core, T.hkv[0], ds, T.kall[:, j * 128:(j + 1) * 128], S["aK%d" % j], NE_HLP)
+                g.wait_ge(S["aV%d" % j], NE_SRC)
+                _send(g, T, topo, core, T.hkv[1], ds, T.vall[:, j * 128:(j + 1) * 128], S["aV%d" % j], NE_HLP)
+                g.wait_ge(S.loc, 2 * NE_HLP)
+        return
+
+    mem = list(T.tables["MEM"])
+    me = mem.index(rank) if rank in mem else None
+    pe, dve, act, sy = g.tensor, g.vector, g.scalar, g.sync
+    A, X, F = AluOpType, AxisListType.X, ActivationFunctionType
+
+    if me is not None:
+        sy.dma_start(T.hkv[0], T.k[:, :]).then_inc(S.sKL, 16)
+        act.dma_start(T.hkv[1], T.v[:, :]).then_inc(S.sVL, 16)
+        sy.dma_start(T.qsb[:, :], T.q[:, :]).then_inc(S.sq, 16)
+        act.dma_start(T.kall[:, me * 128:(me + 1) * 128], T.k[:, :]).then_inc(S["aK%d" % me], 16)
+        sy.dma_start(T.vall[:, me * 128:(me + 1) * 128], T.v[:, :]).then_inc(S["aV%d" % me], 16)
+    else:
+        sy.dma_start(T.qsb[:, :], T.q[:, :]).then_inc(S.sq, 16)
+    dve.memset(T.idn[:, :], 1.0).then_inc(S.sOne, 1)
+
+    if me is not None:
+        groups = plan[me]
+        relays = [c for c, ds in groups[1:]]
+        direct = groups[0][1]
+        g.wait_ge(S.sKL, 16)
+        _send(g, T, topo, core, T.hkv[0], relays, T.hkv[0], S["aK%d" % me], NE_SRC)
+        g.wait_ge(S.sVL, 16)
+        _send(g, T, topo, core, T.hkv[1], relays, T.hkv[1], S["aV%d" % me], NE_SRC)
+        _send(g, T, topo, core, T.hkv[0], direct, T.kall[:, me * 128:(me + 1) * 128], S["aK%d" % me], NE_SRC)
+        _send(g, T, topo, core, T.hkv[1], direct, T.vall[:, me * 128:(me + 1) * 128], S["aV%d" % me], NE_SRC)
+    g.wait_ge(S.sOne, 1)
+    g.affine_select(T.idn[:, :], T.idn[:, :], [[-1, 128]], A.is_equal, 0.0, 0, 1).then_inc(S.sI, 1)
+
+    key, thr = {}, {}
+    for j, groups in enumerate(plan):
+        if j == me:
+            key[j], thr[j] = (0, 0), 16
+            continue
+        for gi, (c, ds) in enumerate(groups):
+            if core in ds:
+                key[j] = (1 if gi == 0 else 2, ds.index(core))
+                thr[j] = NE_SRC if gi == 0 else NE_HLP
+    order = sorted(range(len(plan)), key=lambda j: key[j])
+
+    sf, s, pt, o = [T.sf0, T.sf1], [T.s0, T.s1], [T.pt0, T.pt1], [T.o0, T.o1]
+
+    def col(name, b):
+        i = {"nmF": 0, "nmL": 8, "nm": 16, "w": 24, "lF": 32, "lL": 40}[name] + 4 * b
+        return T.st[:, i:i + 1]
+    L0, R0 = 48, 56
+
+    def sem(n, b):
+        return S[n + str(b)]
+
+    def qb(b):
+        return T.qsb[:, b * 128:(b + 1) * 128]
+
+    def kj(j):
+        return T.kall[:, j * 128:(j + 1) * 128]
+
+    pe.wait_ge(S.sq, 16)
+    pe.wait_ge(S["aK%d" % order[0]], thr[order[0]])
+    for b in range(2):
+        pe.matmul(sf[b][:, 0:128], qb(b), kj(order[0]), True, True).then_inc(sem("sSF", b), 1)
+    for i in range(2):
+        j = order[1 + i]
+        pe.wait_ge(S["aK%d" % j], thr[j])
+        for b in range(2):
+            pe.matmul(s[b][:, i * 128:(i + 1) * 128], qb(b), kj(j), True, True).then_inc(sem("sS", b), 1)
+
+    for b in range(2):
+        dve.wait_ge(sem("sSF", b), 1)
+        dve.tensor_reduce(col("nmF", b), sf[b][:, 0:128], X, A.max, negate=True).then_inc(sem("sMF", b), 1)
+    for b in range(2):
+        dve.wait_ge(sem("sS", b), 2)
+        dve.tensor_reduce(col("nmL", b), s[b][:, 0:256], X, A.max, negate=True).then_inc(sem("sML", b), 1)
+        dve.wait_ge(sem("sML", b), 1)
+        dve.wait_ge(sem("sMF", b), 1)
+        dve.tensor_tensor(col("nm", b), col("nmF", b), col("nmL", b), A.min).then_inc(sem("sM", b), 1)
+
+    for b in range(2):
+        act.wait_ge(sem("sMF", b), 1)
+        act.activation(T.pf[:, b * 128:(b + 1) * 128], sf[b][:, 0:128], F.Exp, bias=col("nmF", b), scale=1.0,
+                       accum_out=col("lF", b)).then_inc(sem("sPF", b), 1)
+    for b in range(2):
+        act.wait_ge(sem("sM", b), 1)
+        act.activation(col("w", b), col("nmF", b), F.Exp, bias=col("nm", b), scale=-1.0).then_inc(sem("sW", b), 1)
+        act.activation(T.p[:, b * 384 + 128:b * 384 + 384], s[b][:, 0:256], F.Exp, bias=col("nm", b), scale=1.0,
+                       accum_out=col("lL", b)).then_inc(sem("sP", b), 1)
+
+    for b in range(2):
+        dve.wait_ge(sem("sW", b), 1)
+        dve.wait_ge(sem("sPF", b), 1)
+        dve.tensor_scalar(T.p[:, b * 384:b * 384 + 128], T.pf[:, b * 128:(b + 1) * 128], col("w", b), None,
+                          A.mult).then_inc(sem("sPS", b), 1)
+
+    pe.wait_ge(S.sI, 1)
+    for b in range(2):
+        pe.wait_ge(sem("sP", b), 1)
+        for i in (1, 2):
+            pe.transpose(pt[b][:, i * 128:(i + 1) * 128], T.p[:, b * 384 + i * 128:b * 384 + (i + 1) * 128],
+                         T.idn[:, :]).then_inc(sem("sT", b), 1)
+        pe.wait_ge(sem("sPS", b), 1)
+        pe.transpose(pt[b][:, 0:128], T.p[:, b * 384:b * 384 + 128], T.idn[:, :]).then_inc(sem("sT", b), 1)
+    for b in range(2):
+        dve.wait_ge(sem("sT", b), 3)
+        dve.tensor_copy(T.pts[:, b * 384:(b + 1) * 384], pt[b][:, 0:384]).then_inc(sem("sC", b), 1)
+        dve.wait_ge(sem("sP", b), 1)
+        dve.tensor_scalar(T.st[:, L0 + b:L0 + b + 1], col("lF", b), col("w", b), col("lL", b), A.mult,
+                          A.add).then_inc(S.sL, 1)
+    dve.wait_ge(S.sL, 2)
+    dve.reciprocal(T.st[:, R0:R0 + 2], T.st[:, L0:L0 + 2]).then_inc(S.sR, 1)
+
+    for i, j in enumerate(order):
+        pe.wait_ge(S["aV%d" % j], thr[j])
+        for b in range(2):
+            if i == 0:
+                pe.wait_ge(sem("sC", b), 1)
+            pe.matmul(o[b][:, 0:128], T.pts[:, b * 384 + i * 128:b * 384 + (i + 1) * 128],
+                      T.vall[:, j * 128:(j + 1) * 128], i == 0, i == 2).then_inc(sem("sO", b), 1)
+
+    dve.wait_ge(S.sR, 1)
+    dve.wait_ge(sem("sO", 0), 3)
+    dve.tensor_scalar(T.ysb[:, 0:128], o[0][:, 0:128], T.st[:, R0:R0 + 1], None, A.mult).then_inc(sem("sY", 0), 1)
+    act.wait_ge(S.sR, 1)
+    act.wait_ge(sem("sO", 1), 3)
+    act.activation(T.ysb[:, 128:256], o[1][:, 0:128], F.Copy, scale=T.st[:, R0 + 1:R0 + 2]).then_inc(sem("sY", 1), 1)
+    sy.wait_ge(sem("sY", 0), 1)
+    sy.dma_start(T.y[0:128, :], T.ysb[:, 0:128]).then_inc(S.sD, 16)
+    act.wait_ge(sem("sY", 1), 1)
+    act.dma_start(T.y[128:256, :], T.ysb[:, 128:256]).then_inc(S.sD, 16)
+
+    if me is not None:
+        g.wait_ge(S.loc, 4 * NE_SRC)
+    g.wait_ge(S.sD, 32)

@@ -5,6 +5,7 @@ NSIM = 256
 NENG = 16
 NE_SRC = 8
 NE_HLP = 8
+SPREAD = False
 
 SCRATCH = {
     "hkv": ("dram", [2, 128, 128], "bfloat16"),
@@ -62,6 +63,34 @@ def _plan(T, topo):
         own = topo.die(s)
         other = [topo.die(c) for c in mates_on_chip if topo.die(c) != own][0]
         port = [c for c in mates_on_chip if all(topo.may_write(c, d) for d in far)]
+        if SPREAD:
+            plain = [c for c in mates_on_chip if c not in port]
+
+            def deal(senders, ds):
+                ds, out = list(ds), []
+                for c in senders:
+                    if not ds:
+                        break
+                    dc = topo.die(c)
+                    d = min(ds, key=lambda x: (cnt.get((x, dc), 0) - cnt.get((x, own + other - dc), 0), ds.index(x)))
+                    ds.remove(d)
+                    cnt[(d, dc)] = cnt.get((d, dc), 0) + 1
+                    out.append((c, [d]))
+                return out, ds
+            alt = lambda cs: [c for pair in zip([c for c in cs if topo.die(c) == own] + [None] * len(cs),
+                                                [c for c in cs if topo.die(c) == other] + [None] * len(cs))
+                              for c in pair if c is not None]
+            if j % 2:
+                near, far = near[::-1], far[::-1]
+            g_far, rest_f = deal(alt(port), far)
+            g_near, rest_n = deal(alt(plain), near)
+            for d in rest_n:
+                cnt[(d, own)] = cnt.get((d, own), 0) + 1
+            if rest_f:
+                for i, d in enumerate(rest_f):
+                    g_far[i % len(g_far)][1].append(d)
+            plan.append([(s, rest_n)] + g_far + g_near)
+            continue
         p_own = [c for c in port if topo.die(c) == own][0]
         p_oth = [c for c in port if topo.die(c) == other][0]
         x_oth = [c for c in mates_on_chip if topo.die(c) == other and c != p_oth and c not in port][0]
@@ -74,7 +103,7 @@ def _plan(T, topo):
     return plan
 
 
-def _send(g, T, topo, core, src, dests, dst_of, sem, ne):
+def _send(g, T, topo, core, src, dests, dst_of, sem, ne, avoid=0):
     m = (1 << NENG) - 1
     ids, dsts = [], []
     for d in dests:
@@ -82,6 +111,8 @@ def _send(g, T, topo, core, src, dests, dst_of, sem, ne):
         rid, pid = topo.addr(d, core)
         ids.append(DstId(rid=rid, pnc=pid))
         dsts.append(dst_of)
+    if sum((m & ~avoid) >> i & 1 for i in range(NENG)) >= ne:
+        m &= ~avoid
     g.remote_dma_fused([RemoteDMATransfer(dst_ids=ids, dma_engine_mask=_pick(m, ne), remote_sem=sem,
                                           srcs=[src], dsts=dsts, alu_op=0)], local_sem=T.sem.loc)
 
@@ -116,16 +147,26 @@ def rank_program(g, core, T, topo):
         sy.dma_start(T.vall[:, me * 128:(me + 1) * 128], T.v[:, :]).then_inc(S["aV%d" % me], 16)
     else:
         sy.dma_start(T.qsb[:, :], T.q[:, :]).then_inc(S.sq, 16)
-    dve.memset(T.idn[:, :], 1.0).then_inc(S.sOne, 1)
+    act.wait_ge(S.sq, 16)
+    act.activation(T.idn[:, :], T.qsb[:, 0:128], F.Exp, scale=0.0).then_inc(S.sOne, 1)
 
     if me is not None:
         groups = plan[me]
         relays = [c for c, ds in groups[1:]]
         direct = groups[0][1]
-        g.wait_ge(S.sKL, 16)
-        _send(g, T, topo, core, T.hkv[0], relays, T.hkv[0], S["aK%d" % me], NE_SRC)
-        g.wait_ge(S.sVL, 16)
-        _send(g, T, topo, core, T.hkv[1], relays, T.hkv[1], S["aV%d" % me], NE_SRC)
+        if SPREAD:
+            off = (1 << NENG) - 1
+            for d in direct:
+                off &= topo.mask(core, d)
+            g.wait_ge(S.sKL, 16)
+            _send(g, T, topo, core, T.hkv[0], relays, T.hkv[0], S["aK%d" % me], NE_SRC, avoid=off)
+            g.wait_ge(S.sVL, 16)
+            _send(g, T, topo, core, T.hkv[1], relays, T.hkv[1], S["aV%d" % me], NE_SRC)
+        else:
+            g.wait_ge(S.sKL, 16)
+            _send(g, T, topo, core, T.hkv[0], relays, T.hkv[0], S["aK%d" % me], NE_SRC)
+            g.wait_ge(S.sVL, 16)
+            _send(g, T, topo, core, T.hkv[1], relays, T.hkv[1], S["aV%d" % me], NE_SRC)
         _send(g, T, topo, core, T.hkv[0], direct, T.kall[:, me * 128:(me + 1) * 128], S["aK%d" % me], NE_SRC)
         _send(g, T, topo, core, T.hkv[1], direct, T.vall[:, me * 128:(me + 1) * 128], S["aV%d" % me], NE_SRC)
     g.wait_ge(S.sOne, 1)
@@ -138,7 +179,7 @@ def rank_program(g, core, T, topo):
             continue
         for gi, (c, ds) in enumerate(groups):
             if core in ds:
-                key[j] = (1 if gi == 0 else 2, ds.index(core))
+                key[j] = (1 if gi == 0 else 2, ds.index(core), gi)
                 thr[j] = NE_SRC if gi == 0 else NE_HLP
     order = sorted(range(len(plan)), key=lambda j: key[j])
 
@@ -153,7 +194,7 @@ def rank_program(g, core, T, topo):
         return S[n + str(b)]
 
     def qb(b):
-        return T.qsb[:, b * 128:(b + 1) * 128]
+        return T.qsb[:, b:256:2]
 
     def kj(j):
         return T.kall[:, j * 128:(j + 1) * 128]
@@ -226,10 +267,9 @@ def rank_program(g, core, T, topo):
     act.wait_ge(sem("sO", 1), 3)
     act.activation(T.ysb[:, 128:256], o[1][:, 0:128], F.Copy, scale=T.st[:, R0 + 1:R0 + 2]).then_inc(sem("sY", 1), 1)
     sy.wait_ge(sem("sY", 0), 1)
-    sy.dma_start(T.y[0:128, :], T.ysb[:, 0:128]).then_inc(S.sD, 16)
-    act.wait_ge(sem("sY", 1), 1)
-    act.dma_start(T.y[128:256, :], T.ysb[:, 128:256]).then_inc(S.sD, 16)
+    sy.wait_ge(sem("sY", 1), 1)
+    sy.dma_start(T.y[:, :], T.ysb[:, :]).then_inc(S.sD, 16)
 
     if me is not None:
         g.wait_ge(S.loc, 4 * NE_SRC)
-    g.wait_ge(S.sD, 32)
+    g.wait_ge(S.sD, 16)

@@ -5,11 +5,15 @@ NSIM = 256
 NENG = 16
 NE_SRC = 8
 NE_HLP = 8
-SPREAD = False
+BIG = 3.0e29
 
 SCRATCH = {
     "hkv": ("dram", [2, 128, 128], "bfloat16"),
     "qsb": ("sbuf", [128, 256], "bfloat16"),
+    "qn": ("sbuf", [128, 256], "bfloat16"),
+    "big": ("sbuf", [128, 256], "bfloat16"),
+    "sc0": ("sbuf", [128, 256], "float32"),
+    "sc1": ("sbuf", [128, 256], "float32"),
     "kall": ("sbuf", [128, 384], "bfloat16"),
     "vall": ("sbuf", [128, 384], "bfloat16"),
     "idn": ("sbuf", [128, 128], "bfloat16"),
@@ -27,9 +31,9 @@ SCRATCH = {
     "o0": ("psum", [128, 512], "float32"),
     "o1": ("psum", [128, 512], "float32"),
 }
-SEMAPHORES = (["sq", "sKL", "sVL", "loc", "sOne", "sI", "sL", "sR", "sD"]
+SEMAPHORES = (["sq", "sQN", "sBig", "sKL", "sVL", "loc", "sOne", "sI", "sL", "sR", "sD"]
               + ["aK%d" % j for j in range(3)] + ["aV%d" % j for j in range(3)]
-              + [n + str(b) for n in ("sSF", "sS", "sMF", "sML", "sM", "sPF", "sW", "sP", "sPS", "sT", "sC", "sO", "sY")
+              + [n + str(b) for n in ("sSF", "sS", "sMF", "sM", "sPF", "sW", "sP", "sPS", "sT", "sC", "sO", "sY")
                  for b in range(2)])
 
 
@@ -63,34 +67,6 @@ def _plan(T, topo):
         own = topo.die(s)
         other = [topo.die(c) for c in mates_on_chip if topo.die(c) != own][0]
         port = [c for c in mates_on_chip if all(topo.may_write(c, d) for d in far)]
-        if SPREAD:
-            plain = [c for c in mates_on_chip if c not in port]
-
-            def deal(senders, ds):
-                ds, out = list(ds), []
-                for c in senders:
-                    if not ds:
-                        break
-                    dc = topo.die(c)
-                    d = min(ds, key=lambda x: (cnt.get((x, dc), 0) - cnt.get((x, own + other - dc), 0), ds.index(x)))
-                    ds.remove(d)
-                    cnt[(d, dc)] = cnt.get((d, dc), 0) + 1
-                    out.append((c, [d]))
-                return out, ds
-            alt = lambda cs: [c for pair in zip([c for c in cs if topo.die(c) == own] + [None] * len(cs),
-                                                [c for c in cs if topo.die(c) == other] + [None] * len(cs))
-                              for c in pair if c is not None]
-            if j % 2:
-                near, far = near[::-1], far[::-1]
-            g_far, rest_f = deal(alt(port), far)
-            g_near, rest_n = deal(alt(plain), near)
-            for d in rest_n:
-                cnt[(d, own)] = cnt.get((d, own), 0) + 1
-            if rest_f:
-                for i, d in enumerate(rest_f):
-                    g_far[i % len(g_far)][1].append(d)
-            plan.append([(s, rest_n)] + g_far + g_near)
-            continue
         p_own = [c for c in port if topo.die(c) == own][0]
         p_oth = [c for c in port if topo.die(c) == other][0]
         x_oth = [c for c in mates_on_chip if topo.die(c) == other and c != p_oth and c not in port][0]
@@ -103,7 +79,7 @@ def _plan(T, topo):
     return plan
 
 
-def _send(g, T, topo, core, src, dests, dst_of, sem, ne, avoid=0):
+def _send(g, T, topo, core, src, dests, dst_of, sem, ne):
     m = (1 << NENG) - 1
     ids, dsts = [], []
     for d in dests:
@@ -111,8 +87,6 @@ def _send(g, T, topo, core, src, dests, dst_of, sem, ne, avoid=0):
         rid, pid = topo.addr(d, core)
         ids.append(DstId(rid=rid, pnc=pid))
         dsts.append(dst_of)
-    if sum((m & ~avoid) >> i & 1 for i in range(NENG)) >= ne:
-        m &= ~avoid
     g.remote_dma_fused([RemoteDMATransfer(dst_ids=ids, dma_engine_mask=_pick(m, ne), remote_sem=sem,
                                           srcs=[src], dsts=dsts, alu_op=0)], local_sem=T.sem.loc)
 
@@ -149,24 +123,18 @@ def rank_program(g, core, T, topo):
         sy.dma_start(T.qsb[:, :], T.q[:, :]).then_inc(S.sq, 16)
     act.wait_ge(S.sq, 16)
     act.activation(T.idn[:, :], T.qsb[:, 0:128], F.Exp, scale=0.0).then_inc(S.sOne, 1)
+    dve.memset(T.big[:, :], BIG).then_inc(S.sBig, 1)
+    dve.wait_ge(S.sq, 16)
+    dve.tensor_scalar(T.qn[:, :], T.qsb[:, :], -1.0, None, A.mult).then_inc(S.sQN, 1)
 
     if me is not None:
         groups = plan[me]
         relays = [c for c, ds in groups[1:]]
         direct = groups[0][1]
-        if SPREAD:
-            off = (1 << NENG) - 1
-            for d in direct:
-                off &= topo.mask(core, d)
-            g.wait_ge(S.sKL, 16)
-            _send(g, T, topo, core, T.hkv[0], relays, T.hkv[0], S["aK%d" % me], NE_SRC, avoid=off)
-            g.wait_ge(S.sVL, 16)
-            _send(g, T, topo, core, T.hkv[1], relays, T.hkv[1], S["aV%d" % me], NE_SRC)
-        else:
-            g.wait_ge(S.sKL, 16)
-            _send(g, T, topo, core, T.hkv[0], relays, T.hkv[0], S["aK%d" % me], NE_SRC)
-            g.wait_ge(S.sVL, 16)
-            _send(g, T, topo, core, T.hkv[1], relays, T.hkv[1], S["aV%d" % me], NE_SRC)
+        g.wait_ge(S.sKL, 16)
+        _send(g, T, topo, core, T.hkv[0], relays, T.hkv[0], S["aK%d" % me], NE_SRC)
+        g.wait_ge(S.sVL, 16)
+        _send(g, T, topo, core, T.hkv[1], relays, T.hkv[1], S["aV%d" % me], NE_SRC)
         _send(g, T, topo, core, T.hkv[0], direct, T.kall[:, me * 128:(me + 1) * 128], S["aK%d" % me], NE_SRC)
         _send(g, T, topo, core, T.hkv[1], direct, T.vall[:, me * 128:(me + 1) * 128], S["aV%d" % me], NE_SRC)
     g.wait_ge(S.sOne, 1)
@@ -183,10 +151,12 @@ def rank_program(g, core, T, topo):
                 thr[j] = NE_SRC if gi == 0 else NE_HLP
     order = sorted(range(len(plan)), key=lambda j: key[j])
 
-    sf, s, pt, o = [T.sf0, T.sf1], [T.s0, T.s1], [T.pt0, T.pt1], [T.o0, T.o1]
+    sf, s, pt, o, sc = [T.sf0, T.sf1], [T.s0, T.s1], [T.pt0, T.pt1], [T.o0, T.o1], [T.sc0, T.sc1]
 
     def col(name, b):
-        i = {"nmF": 0, "nmL": 8, "nm": 16, "w": 24, "lF": 32, "lL": 40}[name] + 4 * b
+        if name == "nm":
+            return sc[b][:, 255:256]
+        i = {"nmF": 0, "w": 24, "lF": 32, "lL": 40}[name] + 4 * b
         return T.st[:, i:i + 1]
     L0, R0 = 48, 56
 
@@ -194,12 +164,12 @@ def rank_program(g, core, T, topo):
         return S[n + str(b)]
 
     def qb(b):
-        return T.qsb[:, b:256:2]
+        return T.qn[:, b:256:2]
 
     def kj(j):
         return T.kall[:, j * 128:(j + 1) * 128]
 
-    pe.wait_ge(S.sq, 16)
+    pe.wait_ge(S.sQN, 1)
     pe.wait_ge(S["aK%d" % order[0]], thr[order[0]])
     for b in range(2):
         pe.matmul(sf[b][:, 0:128], qb(b), kj(order[0]), True, True).then_inc(sem("sSF", b), 1)
@@ -211,22 +181,22 @@ def rank_program(g, core, T, topo):
 
     for b in range(2):
         dve.wait_ge(sem("sSF", b), 1)
-        dve.tensor_reduce(col("nmF", b), sf[b][:, 0:128], X, A.max, negate=True).then_inc(sem("sMF", b), 1)
+        dve.tensor_reduce(col("nmF", b), sf[b][:, 0:128], X, A.min).then_inc(sem("sMF", b), 1)
+    dve.wait_ge(S.sBig, 1)
     for b in range(2):
-        dve.wait_ge(sem("sS", b), 2)
-        dve.tensor_reduce(col("nmL", b), s[b][:, 0:256], X, A.max, negate=True).then_inc(sem("sML", b), 1)
-        dve.wait_ge(sem("sML", b), 1)
         dve.wait_ge(sem("sMF", b), 1)
-        dve.tensor_tensor(col("nm", b), col("nmF", b), col("nmL", b), A.min).then_inc(sem("sM", b), 1)
+        dve.wait_ge(sem("sS", b), 2)
+        dve.tensor_tensor_scan(sc[b][:, 0:256], s[b][:, 0:256], T.big[:, :], col("nmF", b), A.min,
+                               A.min).then_inc(sem("sM", b), 1)
 
     for b in range(2):
         act.wait_ge(sem("sMF", b), 1)
-        act.activation(T.pf[:, b * 128:(b + 1) * 128], sf[b][:, 0:128], F.Exp, bias=col("nmF", b), scale=1.0,
+        act.activation(T.pf[:, b * 128:(b + 1) * 128], sf[b][:, 0:128], F.Exp, bias=col("nmF", b), scale=-1.0,
                        accum_out=col("lF", b)).then_inc(sem("sPF", b), 1)
     for b in range(2):
         act.wait_ge(sem("sM", b), 1)
         act.activation(col("w", b), col("nmF", b), F.Exp, bias=col("nm", b), scale=-1.0).then_inc(sem("sW", b), 1)
-        act.activation(T.p[:, b * 384 + 128:b * 384 + 384], s[b][:, 0:256], F.Exp, bias=col("nm", b), scale=1.0,
+        act.activation(T.p[:, b * 384 + 128:b * 384 + 384], s[b][:, 0:256], F.Exp, bias=col("nm", b), scale=-1.0,
                        accum_out=col("lL", b)).then_inc(sem("sP", b), 1)
 
     for b in range(2):
@@ -252,11 +222,11 @@ def rank_program(g, core, T, topo):
     dve.wait_ge(S.sL, 2)
     dve.reciprocal(T.st[:, R0:R0 + 2], T.st[:, L0:L0 + 2]).then_inc(S.sR, 1)
 
-    for i, j in enumerate(order):
-        pe.wait_ge(S["aV%d" % j], thr[j])
-        for b in range(2):
-            if i == 0:
-                pe.wait_ge(sem("sC", b), 1)
+    for b in range(2):
+        pe.wait_ge(sem("sC", b), 1)
+        for i, j in enumerate(order):
+            if b == 0:
+                pe.wait_ge(S["aV%d" % j], thr[j])
             pe.matmul(o[b][:, 0:128], T.pts[:, b * 384 + i * 128:b * 384 + (i + 1) * 128],
                       T.vall[:, j * 128:(j + 1) * 128], i == 0, i == 2).then_inc(sem("sO", b), 1)
 

@@ -5,13 +5,12 @@ NSIM = 256
 NENG = 16
 NE_SRC = 8
 NE_HLP = 8
-BIG = 3.0e29
 
 SCRATCH = {
     "hkv": ("dram", [2, 128, 128], "bfloat16"),
     "qsb": ("sbuf", [128, 256], "bfloat16"),
     "qn": ("sbuf", [128, 256], "bfloat16"),
-    "big": ("sbuf", [128, 256], "bfloat16"),
+    "one": ("sbuf", [128, 256], "bfloat16"),
     "sc0": ("sbuf", [128, 256], "float32"),
     "sc1": ("sbuf", [128, 256], "float32"),
     "kall": ("sbuf", [128, 384], "bfloat16"),
@@ -31,7 +30,7 @@ SCRATCH = {
     "o0": ("psum", [128, 512], "float32"),
     "o1": ("psum", [128, 512], "float32"),
 }
-SEMAPHORES = (["sq", "sQN", "sBig", "sKL", "sVL", "loc", "sOne", "sI", "sL", "sR", "sD"]
+SEMAPHORES = (["sq", "sQN", "sOne", "sKL", "sVL", "loc", "sFill", "sIo", "sI", "sL", "sR", "sD"]
               + ["aK%d" % j for j in range(3)] + ["aV%d" % j for j in range(3)]
               + [n + str(b) for n in ("sSF", "sS", "sMF", "sM", "sPF", "sW", "sP", "sPS", "sT", "sC", "sO", "sY")
                  for b in range(2)])
@@ -91,8 +90,30 @@ def _send(g, T, topo, core, src, dests, dst_of, sem, ne):
                                           srcs=[src], dsts=dsts, alu_op=0)], local_sem=T.sem.loc)
 
 
+def _wards(T, topo, plan):
+    mem = [T.cores[r] for r in T.tables["MEM"]]
+    recv = [d for d in T.cores if d not in mem]
+    senders = [c for groups in plan for c, ds in groups]
+    reach = {c: [d for d in recv if topo.may_write(c, d)] for c in senders}
+    elig = {d: sum(1 for c in senders if d in reach[c]) for d in recv}
+    got = {d: [] for d in recv}
+    for c in sorted(senders, key=lambda c: len(reach[c])):
+        got[min(reach[c], key=lambda d: (len(got[d]), elig[d]))].append(c)
+    ward = {}
+    for d, cs in got.items():
+        for i, c in enumerate(cs):
+            ward[c] = (d, (128 * i // len(cs)) // 8 * 8, (128 * (i + 1) // len(cs)) // 8 * 8)
+    return ward, {d: len(cs) for d, cs in got.items()}
+
+
+def _identity_cols(g, T, c0, c1):
+    g.affine_select(T.idn[:, c0:c1], T.idn[:, c0:c1], [[-1, c1 - c0]], AluOpType.is_equal, 0.0, -c0,
+                    1).then_inc(T.sem.sIo, 1)
+
+
 def rank_program(g, core, T, topo):
     plan = _plan(T, topo)
+    ward, n_ward = _wards(T, topo, plan)
     S = T.sem
     rank = T.rank_of(core)
 
@@ -101,11 +122,17 @@ def rank_program(g, core, T, topo):
             for c, ds in groups[1:]:
                 if c != core:
                     continue
+                d, c0, c1 = ward[core]
+                g.vector.memset(T.idn[:, c0:c1], 1.0).then_inc(S.sFill, 1)
+                g.wait_ge(S.sFill, 1)
+                _identity_cols(g, T, c0, c1)
+                g.wait_ge(S.sIo, 1)
+                _send(g, T, topo, core, T.idn[:, c0:c1], [d], T.idn[:, c0:c1], S.sI, NE_HLP)
                 g.wait_ge(S["aK%d" % j], NE_SRC)
                 _send(g, T, topo, core, T.hkv[0], ds, T.kall[:, j * 128:(j + 1) * 128], S["aK%d" % j], NE_HLP)
                 g.wait_ge(S["aV%d" % j], NE_SRC)
                 _send(g, T, topo, core, T.hkv[1], ds, T.vall[:, j * 128:(j + 1) * 128], S["aV%d" % j], NE_HLP)
-                g.wait_ge(S.loc, 2 * NE_HLP)
+                g.wait_ge(S.loc, 3 * NE_HLP)
         return
 
     mem = list(T.tables["MEM"])
@@ -122,23 +149,29 @@ def rank_program(g, core, T, topo):
     else:
         sy.dma_start(T.qsb[:, :], T.q[:, :]).then_inc(S.sq, 16)
     act.wait_ge(S.sq, 16)
-    act.activation(T.idn[:, :], T.qsb[:, 0:128], F.Exp, scale=0.0).then_inc(S.sOne, 1)
-    dve.memset(T.big[:, :], BIG).then_inc(S.sBig, 1)
-    dve.wait_ge(S.sq, 16)
-    dve.tensor_scalar(T.qn[:, :], T.qsb[:, :], -1.0, None, A.mult).then_inc(S.sQN, 1)
+    act.activation(T.one[:, :], T.qsb[:, :], F.Exp, scale=0.0).then_inc(S.sOne, 1)
 
     if me is not None:
         groups = plan[me]
         relays = [c for c, ds in groups[1:]]
         direct = groups[0][1]
+        d, c0, c1 = ward[core]
+        dve.memset(T.idn[:, :], 1.0).then_inc(S.sFill, 1)
+        g.wait_ge(S.sFill, 1)
+        _identity_cols(g, T, c0, c1)
+        g.wait_ge(S.sIo, 1)
+        _send(g, T, topo, core, T.idn[:, c0:c1], [d], T.idn[:, c0:c1], S.sI, NE_SRC)
         g.wait_ge(S.sKL, 16)
         _send(g, T, topo, core, T.hkv[0], relays, T.hkv[0], S["aK%d" % me], NE_SRC)
         g.wait_ge(S.sVL, 16)
         _send(g, T, topo, core, T.hkv[1], relays, T.hkv[1], S["aV%d" % me], NE_SRC)
         _send(g, T, topo, core, T.hkv[0], direct, T.kall[:, me * 128:(me + 1) * 128], S["aK%d" % me], NE_SRC)
         _send(g, T, topo, core, T.hkv[1], direct, T.vall[:, me * 128:(me + 1) * 128], S["aV%d" % me], NE_SRC)
-    g.wait_ge(S.sOne, 1)
-    g.affine_select(T.idn[:, :], T.idn[:, :], [[-1, 128]], A.is_equal, 0.0, 0, 1).then_inc(S.sI, 1)
+        rest = [(a, b) for a, b in ((0, c0), (c1, 128)) if b > a]
+        for a, b in rest:
+            _identity_cols(g, T, a, b)
+    dve.wait_ge(S.sq, 16)
+    dve.tensor_scalar(T.qn[:, :], T.qsb[:, :], -1.0, None, A.mult).then_inc(S.sQN, 1)
 
     key, thr = {}, {}
     for j, groups in enumerate(plan):
@@ -182,12 +215,12 @@ def rank_program(g, core, T, topo):
     for b in range(2):
         dve.wait_ge(sem("sSF", b), 1)
         dve.tensor_reduce(col("nmF", b), sf[b][:, 0:128], X, A.min).then_inc(sem("sMF", b), 1)
-    dve.wait_ge(S.sBig, 1)
+    dve.wait_ge(S.sOne, 1)
     for b in range(2):
         dve.wait_ge(sem("sMF", b), 1)
         dve.wait_ge(sem("sS", b), 2)
-        dve.tensor_tensor_scan(sc[b][:, 0:256], s[b][:, 0:256], T.big[:, :], col("nmF", b), A.min,
-                               A.min).then_inc(sem("sM", b), 1)
+        dve.tensor_tensor_scan(sc[b][:, 0:256], s[b][:, 0:256], T.one[:, :], col("nmF", b), A.min,
+                               A.mult).then_inc(sem("sM", b), 1)
 
     for b in range(2):
         act.wait_ge(sem("sMF", b), 1)
@@ -205,7 +238,10 @@ def rank_program(g, core, T, topo):
         dve.tensor_scalar(T.p[:, b * 384:b * 384 + 128], T.pf[:, b * 128:(b + 1) * 128], col("w", b), None,
                           A.mult).then_inc(sem("sPS", b), 1)
 
-    pe.wait_ge(S.sI, 1)
+    if me is None:
+        pe.wait_ge(S.sI, NE_HLP * n_ward[core])
+    else:
+        pe.wait_ge(S.sIo, 1 + len(rest))
     for b in range(2):
         pe.wait_ge(sem("sP", b), 1)
         for i in (1, 2):
@@ -241,5 +277,5 @@ def rank_program(g, core, T, topo):
     sy.dma_start(T.y[:, :], T.ysb[:, :]).then_inc(S.sD, 16)
 
     if me is not None:
-        g.wait_ge(S.loc, 4 * NE_SRC)
+        g.wait_ge(S.loc, 5 * NE_SRC)
     g.wait_ge(S.sD, 16)

@@ -16,6 +16,7 @@ SCRATCH = {
     "kall": ("sbuf", [128, 384], "bfloat16"),
     "vall": ("sbuf", [128, 384], "bfloat16"),
     "idn": ("sbuf", [128, 128], "bfloat16"),
+    "on": ("sbuf", [128, 128], "bfloat16"),
     "pf": ("sbuf", [128, 256], "bfloat16"),
     "p": ("sbuf", [128, 768], "bfloat16"),
     "pts": ("sbuf", [128, 768], "bfloat16"),
@@ -30,7 +31,7 @@ SCRATCH = {
     "o0": ("psum", [128, 512], "float32"),
     "o1": ("psum", [128, 512], "float32"),
 }
-SEMAPHORES = (["sq", "sQN", "sOne", "sKL", "sVL", "loc", "sFill", "sIo", "sI", "sL", "sR", "sD"]
+SEMAPHORES = (["sq", "sQN", "sOne", "sKL", "sVL", "loc", "sFill", "sFo", "sIo", "sI", "sJ", "sL", "sR", "sD"]
               + ["aK%d" % j for j in range(3)] + ["aV%d" % j for j in range(3)]
               + [n + str(b) for n in ("sSF", "sS", "sMF", "sM", "sPF", "sW", "sP", "sPS", "sT", "sC", "sO", "sY")
                  for b in range(2)])
@@ -156,20 +157,27 @@ def rank_program(g, core, T, topo):
         relays = [c for c, ds in groups[1:]]
         direct = groups[0][1]
         d, c0, c1 = ward[core]
+        dve.memset(T.on[:, c0:c1], 1.0).then_inc(S.sFo, 1)
         dve.memset(T.idn[:, :], 1.0).then_inc(S.sFill, 1)
-        g.wait_ge(S.sFill, 1)
-        _identity_cols(g, T, c0, c1)
-        g.wait_ge(S.sIo, 1)
-        _send(g, T, topo, core, T.idn[:, c0:c1], [d], T.idn[:, c0:c1], S.sI, NE_SRC)
+        g.wait_ge(S.sFo, 1)
+        _send(g, T, topo, core, T.on[:, c0:c1], [d], T.idn[:, c0:c1], S.sJ, NE_SRC)
         g.wait_ge(S.sKL, 16)
         _send(g, T, topo, core, T.hkv[0], relays, T.hkv[0], S["aK%d" % me], NE_SRC)
         g.wait_ge(S.sVL, 16)
         _send(g, T, topo, core, T.hkv[1], relays, T.hkv[1], S["aV%d" % me], NE_SRC)
         _send(g, T, topo, core, T.hkv[0], direct, T.kall[:, me * 128:(me + 1) * 128], S["aK%d" % me], NE_SRC)
         _send(g, T, topo, core, T.hkv[1], direct, T.vall[:, me * 128:(me + 1) * 128], S["aV%d" % me], NE_SRC)
-        rest = [(a, b) for a, b in ((0, c0), (c1, 128)) if b > a]
-        for a, b in rest:
-            _identity_cols(g, T, a, b)
+        g.wait_ge(S.sFill, 1)
+        _identity_cols(g, T, 0, 128)
+        n_cut, n_made = 1, 0
+    else:
+        srcs = [T.cores[r] for r in mem]
+        raw = [ward[c][1:] for c in srcs if ward[c][0] == core]
+        n_cut, n_made = len(raw), n_ward[core] - len(raw)
+        if raw:
+            g.wait_ge(S.sJ, NE_SRC * len(raw))
+            for a, b in raw:
+                _identity_cols(g, T, a, b)
     dve.wait_ge(S.sq, 16)
     dve.tensor_scalar(T.qn[:, :], T.qsb[:, :], -1.0, None, A.mult).then_inc(S.sQN, 1)
 
@@ -238,10 +246,10 @@ def rank_program(g, core, T, topo):
         dve.tensor_scalar(T.p[:, b * 384:b * 384 + 128], T.pf[:, b * 128:(b + 1) * 128], col("w", b), None,
                           A.mult).then_inc(sem("sPS", b), 1)
 
-    if me is None:
-        pe.wait_ge(S.sI, NE_HLP * n_ward[core])
-    else:
-        pe.wait_ge(S.sIo, 1 + len(rest))
+    if n_made:
+        pe.wait_ge(S.sI, NE_HLP * n_made)
+    if n_cut:
+        pe.wait_ge(S.sIo, n_cut)
     for b in range(2):
         pe.wait_ge(sem("sP", b), 1)
         for i in (1, 2):

from concourse.bass import DstId, RemoteDMATransfer
from concourse.mybir import AluOpType, AxisListType, ActivationFunctionType

NSIM = 256
NENG = 16
NE_SRC = 8
NE_HLP = 8

SCRATCH = {
    "hkv": ("dram", [2, 128, 128], "bfloat16"),
    "qsb": ("sbuf", [128, 256], "bfloat16"),
    "qn": ("sbuf", [128, 256], "bfloat16"),
    "one": ("sbuf", [128, 256], "bfloat16"),
    "sc0": ("sbuf", [128, 256], "float32"),
    "sc1": ("sbuf", [128, 256], "float32"),
    "kall": ("sbuf", [128, 384], "bfloat16"),
    "vall": ("sbuf", [128, 384], "bfloat16"),
    "idn": ("sbuf", [128, 128], "bfloat16"),
    "on": ("sbuf", [128, 128], "bfloat16"),
    "pf": ("sbuf", [128, 256], "bfloat16"),
    "p": ("sbuf", [128, 768], "bfloat16"),
    "pts": ("sbuf", [128, 768], "bfloat16"),
    "st": ("sbuf", [128, 64], "float32"),
    "ysb": ("sbuf", [128, 256], "bfloat16"),
    "sf0": ("psum", [128, 512], "float32"),
    "sf1": ("psum", [128, 512], "float32"),
    "s0": ("psum", [128, 512], "float32"),
    "s1": ("psum", [128, 512], "float32"),
    "pt0": ("psum", [128, 1024], "bfloat16"),
    "pt1": ("psum", [128, 1024], "bfloat16"),
    "o0": ("psum", [128, 512], "float32"),
    "o1": ("psum", [128, 512], "float32"),
}
SEMAPHORES = (["sq", "sQN", "sOne", "sKL", "sVL", "loc", "sFill", "sFo", "sIo", "sI", "sJ", "sL", "sR", "sD"]
              + ["aK%d" % j for j in range(3)] + ["aV%d" % j for j in range(3)]
              + [n + str(b) for n in ("sSF", "sS", "sMF", "sM", "sPF", "sW", "sP", "sPS", "sT", "sC", "sO", "sY")
                 for b in range(2)])


def _pick(mask, n):
    m = 0
    for i in [i for i in range(NENG) if (mask >> i) & 1][:n]:
        m |= 1 << i
    return m


def _plan(T, topo):
    cores = list(T.cores)
    cnt = {}

    def split(ds, own, other, n_own):
        ds = sorted(ds, key=lambda d: cnt.get((d, own), 0) - cnt.get((d, other), 0))
        a, b = ds[:n_own], ds[n_own:]
        for d in a:
            cnt[(d, own)] = cnt.get((d, own), 0) + 1
        for d in b:
            cnt[(d, other)] = cnt.get((d, other), 0) + 1
        return a, b

    plan = []
    for j, r in enumerate(T.tables["MEM"]):
        s = cores[r]
        mates_on_chip = [c for c in range(NSIM) if c != s and topo.host(c) == topo.host(s)
                         and topo.chip(c) == topo.chip(s) and T.rank_of(c) is None]
        near = [d for d in cores if d != s and topo.may_write(s, d)]
        far = [d for d in cores if d != s and not topo.may_write(s, d)]
        own = topo.die(s)
        other = [topo.die(c) for c in mates_on_chip if topo.die(c) != own][0]
        port = [c for c in mates_on_chip if all(topo.may_write(c, d) for d in far)]
        p_own = [c for c in port if topo.die(c) == own][0]
        p_oth = [c for c in port if topo.die(c) == other][0]
        x_oth = [c for c in mates_on_chip if topo.die(c) == other and c != p_oth and c not in port][0]
        n_a, n_b = split(near, own, other, (len(near) + 1) // 2)
        f_a, f_b = split(far, own, other, (len(far) + 1) // 2)
        groups = [(s, n_a), (p_own, f_a), (p_oth, f_b), (x_oth, n_b)]
        if j % 2:
            groups = [(c, ds[::-1]) for c, ds in groups]
        plan.append([(c, ds) for c, ds in groups if ds or c == s])
    return plan


def _send(g, T, topo, core, src, dests, dst_of, sem, ne):
    m = (1 << NENG) - 1
    ids, dsts = [], []
    for d in dests:
        m &= topo.mask(core, d)
        rid, pid = topo.addr(d, core)
        ids.append(DstId(rid=rid, pnc=pid))
        dsts.append(dst_of)
    g.remote_dma_fused([RemoteDMATransfer(dst_ids=ids, dma_engine_mask=_pick(m, ne), remote_sem=sem,
                                          srcs=[src], dsts=dsts, alu_op=0)], local_sem=T.sem.loc)


def _wards(T, topo, plan):
    mem = [T.cores[r] for r in T.tables["MEM"]]
    recv = [d for d in T.cores if d not in mem]
    senders = [c for groups in plan for c, ds in groups]
    reach = {c: [d for d in recv if topo.may_write(c, d)] for c in senders}
    elig = {d: sum(1 for c in senders if d in reach[c]) for d in recv}
    got = {d: [] for d in recv}
    for c in sorted(senders, key=lambda c: len(reach[c])):
        got[min(reach[c], key=lambda d: (len(got[d]), elig[d]))].append(c)
    ward = {}
    for d, cs in got.items():
        for i, c in enumerate(cs):
            ward[c] = (d, (128 * i // len(cs)) // 8 * 8, (128 * (i + 1) // len(cs)) // 8 * 8)
    return ward, {d: len(cs) for d, cs in got.items()}


def _identity_cols(g, T, c0, c1):
    g.affine_select(T.idn[:, c0:c1], T.idn[:, c0:c1], [[-1, c1 - c0]], AluOpType.is_equal, 0.0, -c0,
                    1).then_inc(T.sem.sIo, 1)


def rank_program(g, core, T, topo):
    plan = _plan(T, topo)
    ward, n_ward = _wards(T, topo, plan)
    S = T.sem
    rank = T.rank_of(core)

    if rank is None:
        for j, groups in enumerate(plan):
            for c, ds in groups[1:]:
                if c != core:
                    continue
                d, c0, c1 = ward[core]
                g.vector.memset(T.idn[:, c0:c1], 1.0).then_inc(S.sFill, 1)
                g.wait_ge(S.sFill, 1)
                _identity_cols(g, T, c0, c1)
                g.wait_ge(S.sIo, 1)
                _send(g, T, topo, core, T.idn[:, c0:c1], [d], T.idn[:, c0:c1], S.sI, NE_HLP)
                g.wait_ge(S["aK%d" % j], NE_SRC)
                _send(g, T, topo, core, T.hkv[0], ds, T.kall[:, j * 128:(j + 1) * 128], S["aK%d" % j], NE_HLP)
                g.wait_ge(S["aV%d" % j], NE_SRC)
                _send(g, T, topo, core, T.hkv[1], ds, T.vall[:, j * 128:(j + 1) * 128], S["aV%d" % j], NE_HLP)
                g.wait_ge(S.loc, 3 * NE_HLP)
        return

    mem = list(T.tables["MEM"])
    me = mem.index(rank) if rank in mem else None
    pe, dve, act, sy = g.tensor, g.vector, g.scalar, g.sync
    A, X, F = AluOpType, AxisListType.X, ActivationFunctionType

    if me is not None:
        sy.dma_start(T.hkv[0], T.k[:, :]).then_inc(S.sKL, 16)
        act.dma_start(T.hkv[1], T.v[:, :]).then_inc(S.sVL, 16)
        sy.dma_start(T.qsb[:, :], T.q[:, :]).then_inc(S.sq, 16)
        act.dma_start(T.kall[:, me * 128:(me + 1) * 128], T.k[:, :]).then_inc(S["aK%d" % me], 16)
        sy.dma_start(T.vall[:, me * 128:(me + 1) * 128], T.v[:, :]).then_inc(S["aV%d" % me], 16)
    else:
        sy.dma_start(T.qsb[:, :], T.q[:, :]).then_inc(S.sq, 16)
    act.wait_ge(S.sq, 16)
    act.activation(T.one[:, :], T.qsb[:, :], F.Exp, scale=0.0).then_inc(S.sOne, 1)

    if me is not None:
        groups = plan[me]
        relays = [c for c, ds in groups[1:]]
        direct = groups[0][1]
        d, c0, c1 = ward[core]
        dve.memset(T.on[:, c0:c1], 1.0).then_inc(S.sFo, 1)
        dve.memset(T.idn[:, :], 1.0).then_inc(S.sFill, 1)
        g.wait_ge(S.sFo, 1)
        _send(g, T, topo, core, T.on[:, c0:c1], [d], T.idn[:, c0:c1], S.sJ, NE_SRC)
        g.wait_ge(S.sKL, 16)
        _send(g, T, topo, core, T.hkv[0], relays, T.hkv[0], S["aK%d" % me], NE_SRC)
        g.wait_ge(S.sVL, 16)
        _send(g, T, topo, core, T.hkv[1], relays, T.hkv[1], S["aV%d" % me], NE_SRC)
        _send(g, T, topo, core, T.hkv[0], direct, T.kall[:, me * 128:(me + 1) * 128], S["aK%d" % me], NE_SRC)
        _send(g, T, topo, core, T.hkv[1], direct, T.vall[:, me * 128:(me + 1) * 128], S["aV%d" % me], NE_SRC)
        g.wait_ge(S.sFill, 1)
        _identity_cols(g, T, 0, 128)
        n_cut, n_made = 1, 0
    else:
        srcs = [T.cores[r] for r in mem]
        raw = [ward[c][1:] for c in srcs if ward[c][0] == core]
        n_cut, n_made = len(raw), n_ward[core] - len(raw)
        if raw:
            g.wait_ge(S.sJ, NE_SRC * len(raw))
            for a, b in raw:
                _identity_cols(g, T, a, b)
    dve.wait_ge(S.sq, 16)
    dve.tensor_scalar(T.qn[:, :], T.qsb[:, :], -1.0, None, A.mult).then_inc(S.sQN, 1)

    key, thr = {}, {}
    for j, groups in enumerate(plan):
        if j == me:
            key[j], thr[j] = (0, 0), 16
            continue
        for gi, (c, ds) in enumerate(groups):
            if core in ds:
                key[j] = (1 if gi == 0 else 2, ds.index(core), gi)
                thr[j] = NE_SRC if gi == 0 else NE_HLP
    order = sorted(range(len(plan)), key=lambda j: key[j])

    sf, s, pt, o, sc = [T.sf0, T.sf1], [T.s0, T.s1], [T.pt0, T.pt1], [T.o0, T.o1], [T.sc0, T.sc1]

    def col(name, b):
        if name == "nm":
            return sc[b][:, 255:256]
        i = {"nmF": 0, "w": 24, "lF": 32, "lL": 40}[name] + 4 * b
        return T.st[:, i:i + 1]
    L0, R0 = 48, 56

    def sem(n, b):
        return S[n + str(b)]

    def qb(b):
        return T.qn[:, b:256:2]

    def kj(j):
        return T.kall[:, j * 128:(j + 1) * 128]

    pe.wait_ge(S.sQN, 1)
    pe.wait_ge(S["aK%d" % order[0]], thr[order[0]])
    for b in range(2):
        pe.matmul(sf[b][:, 0:128], qb(b), kj(order[0]), True, True).then_inc(sem("sSF", b), 1)
    for i in range(2):
        j = order[1 + i]
        pe.wait_ge(S["aK%d" % j], thr[j])
        for b in range(2):
            pe.matmul(s[b][:, i * 128:(i + 1) * 128], qb(b), kj(j), True, True).then_inc(sem("sS", b), 1)

    for b in range(2):
        dve.wait_ge(sem("sSF", b), 1)
        dve.tensor_reduce(col("nmF", b), sf[b][:, 0:128], X, A.min).then_inc(sem("sMF", b), 1)
    dve.wait_ge(S.sOne, 1)
    for b in range(2):
        dve.wait_ge(sem("sMF", b), 1)
        dve.wait_ge(sem("sS", b), 2)
        dve.tensor_tensor_scan(sc[b][:, 0:256], s[b][:, 0:256], T.one[:, :], col("nmF", b), A.min,
                               A.mult).then_inc(sem("sM", b), 1)

    for b in range(2):
        act.wait_ge(sem("sMF", b), 1)
        act.activation(T.pf[:, b * 128:(b + 1) * 128], sf[b][:, 0:128], F.Exp, bias=col("nmF", b), scale=-1.0,
                       accum_out=col("lF", b)).then_inc(sem("sPF", b), 1)
    for b in range(2):
        act.wait_ge(sem("sM", b), 1)
        act.activation(col("w", b), col("nmF", b), F.Exp, bias=col("nm", b), scale=-1.0).then_inc(sem("sW", b), 1)
        act.activation(T.p[:, b * 384 + 128:b * 384 + 384], s[b][:, 0:256], F.Exp, bias=col("nm", b), scale=-1.0,
                       accum_out=col("lL", b)).then_inc(sem("sP", b), 1)

    for b in range(2):
        dve.wait_ge(sem("sW", b), 1)
        dve.wait_ge(sem("sPF", b), 1)
        dve.tensor_scalar(T.p[:, b * 384:b * 384 + 128], T.pf[:, b * 128:(b + 1) * 128], col("w", b), None,
                          A.mult).then_inc(sem("sPS", b), 1)

    if n_made:
        pe.wait_ge(S.sI, NE_HLP * n_made)
    if n_cut:
        pe.wait_ge(S.sIo, n_cut)
    for b in range(2):
        pe.wait_ge(sem("sP", b), 1)
        for i in (1, 2):
            pe.transpose(pt[b][:, i * 128:(i + 1) * 128], T.p[:, b * 384 + i * 128:b * 384 + (i + 1) * 128],
                         T.idn[:, :]).then_inc(sem("sT", b), 1)
        pe.wait_ge(sem("sPS", b), 1)
        pe.transpose(pt[b][:, 0:128], T.p[:, b * 384:b * 384 + 128], T.idn[:, :]).then_inc(sem("sT", b), 1)
    for b in range(2):
        dve.wait_ge(sem("sT", b), 3)
        dve.tensor_copy(T.pts[:, b * 384:(b + 1) * 384], pt[b][:, 0:384]).then_inc(sem("sC", b), 1)
        dve.wait_ge(sem("sP", b), 1)
        dve.tensor_scalar(T.st[:, L0 + b:L0 + b + 1], col("lF", b), col("w", b), col("lL", b), A.mult,
                          A.add).then_inc(S.sL, 1)
    dve.wait_ge(S.sL, 2)
    dve.reciprocal(T.st[:, R0:R0 + 2], T.st[:, L0:L0 + 2]).then_inc(S.sR, 1)

    for b in range(2):
        pe.wait_ge(sem("sC", b), 1)
        for i, j in enumerate(order):
            if b == 0:
                pe.wait_ge(S["aV%d" % j], thr[j])
            pe.matmul(o[b][:, 0:128], T.pts[:, b * 384 + i * 128:b * 384 + (i + 1) * 128],
                      T.vall[:, j * 128:(j + 1) * 128], i == 0, i == 2).then_inc(sem("sO", b), 1)

    dve.wait_ge(S.sR, 1)
    dve.wait_ge(sem("sO", 0), 3)
    dve.tensor_scalar(T.ysb[:, 0:128], o[0][:, 0:128], T.st[:, R0:R0 + 1], None, A.mult).then_inc(sem("sY", 0), 1)
    act.wait_ge(S.sR, 1)
    act.wait_ge(sem("sO", 1), 3)
    act.activation(T.ysb[:, 128:256], o[1][:, 0:128], F.Copy, scale=T.st[:, R0 + 1:R0 + 2]).then_inc(sem("sY", 1), 1)
    sy.wait_ge(sem("sY", 0), 1)
    sy.wait_ge(sem("sY", 1), 1)
    sy.dma_start(T.y[:, :], T.ysb[:, :]).then_inc(S.sD, 16)

    if me is not None:
        g.wait_ge(S.loc, 5 * NE_SRC)
    g.wait_ge(S.sD, 16)
